import numpy as np
import ml_dtypes


def mxq(x, axis, fmt="e4m3"):
    dtype, down = {"e4m3": (ml_dtypes.float8_e4m3fn, 7), "e5m2": (ml_dtypes.float8_e5m2, 14)}[fmt]
    v = np.moveaxis(np.asarray(x, np.float32).astype(ml_dtypes.bfloat16).astype(np.float64), axis, -1)
    blocks = v.reshape(v.shape[:-1] + (-1, 32))
    amax = np.abs(blocks).max(-1, keepdims=True)
    byte = np.maximum(np.where(amax > 0, np.frexp(amax)[1] - 1 + 127, 0) - down, 1)
    scale = np.exp2(byte - 127.0)
    codes = (blocks / scale).astype(np.float32).astype(dtype).astype(np.float64)
    return np.moveaxis((codes * scale).reshape(v.shape), -1, axis)


WIDE = False


def mx_kscale(k):
    if not WIDE:
        return np.ones(k)
    levels = np.array([10, -10, 5, -5, 0])
    if k % 512:
        return np.exp2(np.random.permutation(np.resize(levels, k // 32))).repeat(32)
    a = np.empty((k // 512, 16))
    for p in range(k // 512):
        a[p, :8] = np.random.permutation(np.resize(levels, 8))
        for g in range(8):
            far = levels[np.abs(levels - a[p, g]) >= 10]
            a[p, g + 8] = far[np.random.randint(len(far))]
    return np.exp2(a.ravel()).repeat(32)


def f64(x):
    return np.asarray(x).astype(np.float64)


def striped(idx):
    return np.tile(idx.reshape(-1, 16).T, (8, 1)).astype(np.uint16)


def unstriped(offs):
    return offs[:16].T.reshape(-1).astype(np.int64)


E2M1 = np.array([0.0, 0.5, 1.0, 1.5, 2.0, 3.0, 4.0, 6.0, -0.0, -0.5, -1.0, -1.5, -2.0, -3.0, -4.0, -6.0])


def pack_weight(w, fmt):
    k, n = w.shape
    w = f64(np.asarray(w, np.float32).astype(ml_dtypes.bfloat16)).reshape(k // 32, 32, n)
    amax = np.abs(w).max(1)
    if fmt == "e4m3":
        byte = np.frexp(amax)[1] - 1 + 127 - 7
    else:
        mant, ex = np.frexp(amax / 6.0)
        byte = np.where(mant > 0.5, ex, ex - 1) + 127
    byte = np.clip(np.where(amax > 0, byte, 1), 1, 254)
    scaled = (w * np.exp2(127.0 - byte)[:, None, :]).reshape(k, n).astype(np.float32)
    by_word = np.ascontiguousarray(scaled.reshape(k // 512, 128, 4, n).transpose(0, 1, 3, 2))
    if fmt == "e4m3":
        words = by_word.astype(ml_dtypes.float8_e4m3fn).view(np.uint8)
    else:
        c = by_word.astype(ml_dtypes.float4_e2m1fn).view(np.uint8) & 0xF
        words = (c[..., 0::2] | (c[..., 1::2] << 4)).reshape(k // 512, 128, 2 * n)
    return np.ascontiguousarray(words), np.ascontiguousarray(byte.astype(np.uint8).reshape(k // 512, 16, n))


def unpack_weight(words, scales, fmt):
    g, _, n = scales.shape
    words = np.ascontiguousarray(words).reshape(g, 128, n, -1)
    if fmt == "e4m3":
        vals = words.view(ml_dtypes.float8_e4m3fn).astype(np.float64)
    else:
        nib = np.empty((g, 128, n, 4), np.uint8)
        nib[..., 0::2] = words & 0xF
        nib[..., 1::2] = words >> 4
        vals = E2M1[nib]
    vals = vals * np.repeat(np.exp2(scales.astype(np.float64) - 127.0), 8, axis=1)[..., None]
    return vals.transpose(0, 1, 3, 2).reshape(g * 512, n)


def gelu(v):
    return 0.5 * v * (1.0 + np.tanh(np.sqrt(2.0 / np.pi) * (v + 0.044715 * v**3)))


K, H, T, S, T2, P = 1024, 1024, 2048, 512, 1024, 512

def setup_inputs():
    n = np.random.standard_normal
    s = mx_kscale(K)[:, None]
    u = mx_kscale(H)[:, None]
    d = {}
    d["tab_words"], d["tab_scales"] = pack_weight(n((K, T)) * s, "e4m3")
    d["offs"] = striped(np.random.permutation(T)[:S])
    d["w1"] = (0.8 * n((K, H)) / K ** 0.5 / s * np.sqrt(u.T)).astype(np.float32)
    d["wd_words"], d["wd_scales"] = pack_weight(0.8 * n((K, H)) / K ** 0.5 / s * u.T, "e2m1")
    d["page0"] = (n((H, T2)) * u).astype(np.float32)
    d["wgs"] = np.exp(0.3 * n((128, S))).astype(np.float32)
    d["offs2"] = striped(np.random.permutation(T2)[:S])
    d["offs3"] = striped(np.random.permutation(T2)[:P])
    d["show"] = np.exp(0.4 * n((H, P))).astype(np.float32)
    d["low"] = ((0.4 * n(H) - 0.2) * u[:, 0]).astype(np.float32)
    d["vec"] = (0.8 * n(H) / H ** 0.5 / u[:, 0] ** 2).astype(np.float32)
    d["slot"] = (0.8 + 0.6 * n(T2)).astype(np.float32)
    return d

def reference(tab_words, tab_scales, offs, w1, wd_words, wd_scales, page0, wgs, offs2, offs3, show, low, vec, slot):
    v = unpack_weight(tab_words, tab_scales, "e4m3")[:, unstriped(offs)]
    first = mxq(f64(w1), 0, "e4m3").T @ v
    second = unpack_weight(wd_words, wd_scales, "e2m1").T @ v
    h = np.square(first) - second
    page = f64(page0).copy()
    page[:, unstriped(offs2)] = np.tile(f64(wgs), (H // 128, 1)) * h
    x = page[:, unstriped(offs3)] * f64(show)
    x = np.maximum(x, f64(low)[:, None]) * f64(vec)[:, None]
    e = mxq(page, 0, "e4m3").T @ mxq(x, 0, "e4m3")
    return np.exp(np.minimum(e, f64(slot)[:, None]))

@@ -1,0 +1,345 @@
+from contextlib import ExitStack
+
+import concourse.mybir as mybir
+
+K, H, T, S, T2, PJ = 1024, 1024, 2048, 512, 1024, 512
+FLOPS = 3221225472
+
+F32 = mybir.dt.float32
+BF16 = mybir.dt.bfloat16
+I32 = mybir.dt.int32
+U32 = mybir.dt.uint32
+U16 = mybir.dt.uint16
+U8 = mybir.dt.uint8
+FP8X4 = mybir.dt.float8_e4m3fn_x4
+FP4X4 = mybir.dt.float4_e2m1fn_x4
+ALU = mybir.AluOpType
+ACT = mybir.ActivationFunctionType
+
+P = 128
+
+
+def tile_list_bonsai_vigour_page_kernel(
+    tc, tab_words, tab_scales, offs, w1, wd_words, wd_scales, page0, wgs, offs2, offs3, show, low, vec, slot, out
+):
+    nc = tc.nc
+    with ExitStack() as ctx:
+        lists = ctx.enter_context(tc.tile_pool(name="lists", bufs=1))
+        keep = ctx.enter_context(tc.tile_pool(name="keep", bufs=1))
+        ring = ctx.enter_context(tc.tile_pool(name="ring", bufs=3))
+        psum = ctx.enter_context(tc.psum_pool(name="psum", bufs=1))
+
+        def held(shape, dtype, name, tag=None):
+            return keep.tile(shape, dtype, name=name, tag=tag or name, align_bytes=64)
+
+        o1 = lists.tile([P, S // 16], U16, name="o1")
+        o2 = lists.tile([P, S // 16], U16, name="o2")
+        o3 = lists.tile([P, PJ // 16], U16, name="o3")
+        wds_raw = held([P, 2 * H], U8, "wds_raw")
+        tabs = held([P, 2 * T], U8, "tabs")
+        warm_in = held([P, 1], F32, "warm_in")
+        warm_out = held([P, 1], F32, "warm_out")
+        nc.vector.memset(tabs[:, :T].bitcast(I32), 0)
+        nc.gpsimd.memset(tabs[:, T:].bitcast(I32), 0)
+        nc.gpsimd.memset(wds_raw[:].bitcast(I32), 0)
+        nc.vector.memset(warm_in[:], 0.0)
+        nc.scalar.activation(out=warm_out[:], in_=warm_in[:], func=ACT.Exp)
+
+        tabw = [held([P, T], U32, "tabw%d" % a) for a in range(2)]
+        w1raw = {(a, b): held([P, 4, 512], F32, "w1raw%d%d" % (a, b)) for a in range(2) for b in range(2)}
+        wdw_raw = held([P, 4 * H], U8, "wdw_raw")
+        page = [held([P, T2], F32, "page%d" % n) for n in range(8)]
+        shw = [held([P, PJ], F32, "show%d" % n) for n in range(8)]
+        gain0 = held([P, S], F32, "gain0")
+        gain123 = held([P, 3, S], F32, "gain123")
+        low_t = held([P, 2, 4], F32, "low_t")
+        vec_t = held([P, 2, 4], F32, "vec_t")
+        slot_t = held([P, 8], F32, "slot_t")
+
+        page_rows = page0.rearrange("(b p t) m -> b t p m", b=2, t=4)
+        show_rows = show.rearrange("(b p t) j -> b t p j", b=2, t=4)
+        wgs_rows = wgs.rearrange("(p t) j -> p t j", t=4)
+        tab_sc32 = tab_scales.bitcast(I32)
+        wd_sc32 = wd_scales.bitcast(I32)
+
+        def load_tabw(a):
+            nc.sync.dma_start(out=tabw[a][:].bitcast(I32), in_=tab_words[a].rearrange("p n t -> p (n t)").bitcast(I32))
+
+        def load_w1(a, b):
+            nc.sync.dma_start(
+                out=w1raw[a, b][:],
+                in_=w1[512 * a : 512 * (a + 1), 512 * b : 512 * (b + 1)].rearrange("(p j) c -> p j c", j=4),
+            )
+
+        def load_page(n):
+            nc.sync.dma_start(out=page[n][:], in_=page_rows[n // 4, n % 4])
+
+        def load_show(n):
+            nc.sync.dma_start(out=shw[n][:], in_=show_rows[n // 4, n % 4])
+
+        for q in range(4):
+            nc.gpsimd.dma_start(
+                out=wds_raw[32 * q : 32 * q + 4, :].bitcast(I32).rearrange("r (a c) -> r a c", a=2),
+                in_=wd_sc32[:, 4 * q : 4 * q + 4, :].rearrange("a r c -> r a c"),
+            )
+
+        nc.sync.dma_start(o1[:], offs)
+        nc.sync.dma_start(o2[:], offs2)
+        nc.sync.dma_start(o3[:], offs3)
+        nc.sync.dma_start(out=low_t[:], in_=low.rearrange("(b p t) -> p b t", b=2, t=4))
+        nc.sync.dma_start(out=vec_t[:], in_=vec.rearrange("(b p t) -> p b t", b=2, t=4))
+        nc.sync.dma_start(
+            out=wdw_raw[:].bitcast(I32).rearrange("p (a c) -> p a c", a=2),
+            in_=wd_words.bitcast(I32).rearrange("a p c -> p a c"),
+        )
+        load_tabw(0)
+        for q in range(4):
+            nc.sync.dma_start(
+                out=tabs[32 * q : 32 * q + 4, :].bitcast(I32).rearrange("r (a c) -> r a c", a=2),
+                in_=tab_sc32[:, 4 * q : 4 * q + 4, :].rearrange("a r c -> r a c"),
+            )
+        load_tabw(1)
+        load_w1(0, 0)
+        load_w1(1, 0)
+        load_page(0)
+        for q in (0, 2, 1, 3):
+            nc.sync.dma_start(out=gain0[32 * q : 32 * q + 32, :], in_=wgs_rows[:, 0, :])
+        load_show(0)
+        for q in (0, 2, 1, 3):
+            nc.sync.dma_start(out=gain123[32 * q : 32 * q + 32, :, :], in_=wgs_rows[:, 1:4, :])
+        load_page(1)
+        load_w1(0, 1)
+        load_show(1)
+        load_page(2)
+        load_w1(1, 1)
+        load_show(2)
+        for n in range(3, 8):
+            load_page(n)
+            load_show(n)
+        with nc.allow_non_contiguous_dma(reason="one value a partition"):
+            nc.sync.dma_start(out=slot_t[:], in_=slot.rearrange("(c p) -> p c", p=P))
+
+        vw = [held([P, S], U32, "vw%d" % a) for a in range(2)]
+        vs = [held([P, S], U8, "vs%d" % a) for a in range(2)]
+        wdw = held([P, 4 * H], U8, "wdw")
+        wds = held([P, 2 * H], U8, "wds", "tabw0")
+        nc.vector.tensor_copy(
+            out=wdw[:].bitcast(U16).rearrange("p (g t m) -> p g t m", g=4, t=4),
+            in_=wdw_raw[:].bitcast(U16).rearrange("p (g m t) -> p g t m", g=4, t=4),
+        )
+        nc.vector.tensor_copy(vw[0][:], tabw[0][:].indirect(o1[:]))
+        nc.vector.tensor_copy(vs[0][:], tabs[:, :T].indirect(o1[:]))
+        nc.vector.tensor_copy(
+            out=wds[:].rearrange("p (g t m) -> p g t m", g=4, t=4),
+            in_=wds_raw[:].rearrange("p (g m t) -> p g t m", g=4, t=4),
+        )
+        nc.vector.tensor_copy(vs[1][:], tabs[:, T:].indirect(o1[:]))
+        nc.vector.tensor_copy(vw[1][:], tabw[1][:].indirect(o1[:]))
+
+        w1c = {}
+        w1s = {}
+
+        def w1_piece(a, b, t0, t1, engine, tag=None):
+            nt = t1 - t0
+            name = "%d%d%d" % (a, b, t0)
+            stage = held([P, nt * 512], BF16, "w1bf" + name, tag)
+            src = w1raw[a, b][:].rearrange("p j (m t) -> p m j t", t=4)[:, :, :, t0:t1]
+            dst = stage[:].rearrange("p (t m j) -> p m j t", t=nt, j=4)
+            if engine == "scalar":
+                nc.scalar.copy(out=dst, in_=src)
+            else:
+                nc.vector.tensor_copy(out=dst, in_=src)
+
+            def quant(c0, c1):
+                codes = held([P, (c1 - c0) * P], U32, "w1c%s%d" % (name, c0))
+                scales = held([P, (c1 - c0) * P], U8, "w1s%s%d" % (name, c0))
+                nc.vector.quantize_mx(
+                    out=codes[:].bitcast(FP8X4), scales=scales[:], in_=stage[:, (c0 - t0) * 512 : (c1 - t0) * 512]
+                )
+                for t in range(c0, c1):
+                    w1c[a, b, t] = codes[:, (t - c0) * P : (t - c0 + 1) * P]
+                    w1s[a, b, t] = scales[:, (t - c0) * P : (t - c0 + 1) * P]
+
+            return quant
+
+        banks = {}
+        sq = {}
+        hh = {}
+        yy = {}
+
+        def second_product(n, passes=(0, 1)):
+            b, t = divmod(n, 4)
+            if n not in banks:
+                banks[n] = psum.tile([P, S], F32, name="second%d" % n, tag="bank%d" % ((2 * n + 1) % 8))
+            second = banks[n]
+            for a in passes:
+                g = (2 * a + b) * 4 + t
+                nc.tensor.matmul_mx(
+                    out=second[:],
+                    lhsT=wdw[:, 256 * g : 256 * (g + 1)].bitcast(FP4X4),
+                    lhsT_scale=wds[:, P * g : P * (g + 1)],
+                    rhs=vw[a][:].bitcast(FP8X4),
+                    rhs_scale=vs[a][:],
+                    start=(a == 0),
+                    stop=(a == 1),
+                )
+
+        def first_product(n):
+            b, t = divmod(n, 4)
+            first = psum.tile([P, S], F32, name="first%d" % n, tag="bank%d" % (2 * n % 8))
+            for a in range(2):
+                nc.tensor.matmul_mx(
+                    out=first[:],
+                    lhsT=w1c[a, b, t].bitcast(FP8X4),
+                    lhsT_scale=w1s[a, b, t],
+                    rhs=vw[a][:].bitcast(FP8X4),
+                    rhs_scale=vs[a][:],
+                    start=(a == 0),
+                    stop=(a == 1),
+                )
+            sq[n] = ring.tile([P, S], F32, name="sq%d" % n, tag="sq", bufs=4, align_bytes=64)
+            nc.scalar.activation(out=sq[n][:], in_=first[:], func=ACT.Square)
+
+        h_tags = ["hA", "hB", "hA", "hB", "hA", "hB", "pgbf0", "xil0"]
+
+        def sub(n):
+            hh[n] = held([P, S], F32, "h%d" % n, h_tags[n])
+            nc.vector.tensor_tensor(out=hh[n][:], in0=sq[n][:], in1=banks[n][:], op=ALU.subtract)
+
+        def scatter(n):
+            t = n % 4
+            gain = gain0[:] if t == 0 else gain123[:, t - 1, :]
+            nc.vector.tensor_tensor(page[n][:].indirect(o2[:]), hh[n][:], gain, ALU.mult)
+
+        pgbf = [held([P, 4 * T2], BF16, "pgbf%d" % b) for b in range(2)]
+
+        def page_round(n, c0, c1):
+            b, t = divmod(n, 4)
+            dst = pgbf[b][:].rearrange("p (m t) -> p t m", t=4)
+            nc.scalar.copy(out=dst[:, t, c0:c1], in_=page[n][:, c0:c1])
+
+        pcodes = {}
+        pscales = {}
+
+        def page_quant(b, c0, c1):
+            codes = held([P, c1 - c0], U32, "pc%d_%d" % (b, c0))
+            scales = held([P, c1 - c0], U8, "ps%d_%d" % (b, c0))
+            nc.vector.quantize_mx(out=codes[:].bitcast(FP8X4), scales=scales[:], in_=pgbf[b][:, 4 * c0 : 4 * c1])
+            for c in range(c0 // P, c1 // P):
+                pcodes[b, c] = codes[:, c * P - c0 : (c + 1) * P - c0]
+                pscales[b, c] = scales[:, c * P - c0 : (c + 1) * P - c0]
+
+        def gather(n):
+            yy[n] = ring.tile([P, PJ], F32, name="y%d" % n, tag="y", align_bytes=64)
+            nc.vector.tensor_tensor(yy[n][:], page[n][:].indirect(o3[:]), shw[n][:], ALU.mult)
+
+        xst = [held([P, 4, PJ], BF16, "xst%d" % b) for b in range(2)]
+        xil = [held([P, 4 * PJ], BF16, "xil%d" % b) for b in range(2)]
+        xc = [held([P, PJ], U32, "xc%d" % b) for b in range(2)]
+        xs = [held([P, PJ], U8, "xs%d" % b) for b in range(2)]
+
+        def floor_scale(n):
+            b, t = divmod(n, 4)
+            nc.vector.tensor_scalar(
+                out=xst[b][:, t, :],
+                in0=yy[n][:],
+                scalar1=low_t[:, b, t : t + 1],
+                scalar2=vec_t[:, b, t : t + 1],
+                op0=ALU.max,
+                op1=ALU.mult,
+            )
+
+        def x_weave(b, engine):
+            dst = xil[b][:].rearrange("p (c i t) -> p c t i", i=4, t=4)
+            src = xst[b][:].rearrange("p t (c i) -> p c t i", i=4)
+            if engine == "scalar":
+                nc.scalar.copy(out=dst, in_=src)
+            else:
+                nc.vector.tensor_copy(out=dst, in_=src)
+
+        def x_quant(b):
+            nc.vector.quantize_mx(out=xc[b][:].bitcast(FP8X4), scales=xs[b][:], in_=xil[b][:])
+
+        ebank = {}
+
+        def final_pass(b, c):
+            if b == 0:
+                ebank[c] = psum.tile([P, PJ], F32, name="e%d" % c, tag="bank%d" % c)
+            nc.tensor.matmul_mx(
+                out=ebank[c][:],
+                lhsT=pcodes[b, c].bitcast(FP8X4),
+                lhsT_scale=pscales[b, c],
+                rhs=xc[b][:].bitcast(FP8X4),
+                rhs_scale=xs[b][:],
+                start=(b == 0),
+                stop=(b == 1),
+            )
+
+        def epilogue(c):
+            mn = ring.tile([P, PJ], F32, name="mn%d" % c, tag="y", align_bytes=64)
+            nc.vector.tensor_scalar(
+                out=mn[:], in0=ebank[c][:], scalar1=slot_t[:, c : c + 1], scalar2=None, op0=ALU.min
+            )
+            ex = ring.tile([P, PJ], F32, name="ex%d" % c, tag="sq", bufs=4, align_bytes=64)
+            nc.scalar.activation(out=ex[:], in_=mn[:], func=ACT.Exp)
+            nc.sync.dma_start(out=out[c * P : (c + 1) * P, :], in_=ex[:])
+
+        for n in range(4):
+            second_product(n, (0,))
+        second_product(0, (1,))
+        q00a = w1_piece(0, 0, 0, 1, "scalar")
+        q00b = w1_piece(0, 0, 1, 4, "scalar")
+        q00a(0, 1)
+        q10a = w1_piece(1, 0, 0, 1, "vector", "wds_raw")
+        q10a(0, 1)
+        first_product(0)
+        q10b = w1_piece(1, 0, 1, 4, "vector")
+        q00b(1, 2)
+        q10b(1, 2)
+        second_product(1, (1,))
+        first_product(1)
+        sub(0)
+        later = {}
+        for n in range(8):
+            scatter(n)
+            if n == 0:
+                q00b(2, 4)
+                q10b(2, 4)
+                for m in (2, 3):
+                    second_product(m, (1,))
+                    first_product(m)
+            if n < 2:
+                later[n] = w1_piece(n, 1, 0, 4, "scalar", h_tags[n])
+            if n in (1, 2):
+                later[n - 1](0, 4)
+            if 2 <= n < 6:
+                second_product(n + 2)
+                first_product(n + 2)
+            if n == 4:
+                page_quant(0, 0, T2)
+            if n == 5:
+                x_quant(0)
+            if n + 1 < 8:
+                sub(n + 1)
+            if n < 7:
+                page_round(n, 0, T2)
+            else:
+                for c in range(4):
+                    page_round(n, 256 * c, 256 * (c + 1))
+            gather(n)
+            if n > 0:
+                floor_scale(n - 1)
+            if n == 4:
+                x_weave(0, "scalar")
+        for c in range(8):
+            final_pass(0, c)
+        page_quant(1, 0, 256)
+        floor_scale(7)
+        page_quant(1, 256, 512)
+        x_weave(1, "vector")
+        page_quant(1, 512, 768)
+        x_quant(1)
+        page_quant(1, 768, 1024)
+        for c in range(8):
+            final_pass(1, c)
+            epilogue(c)

@@ -41,7 +41,7 @@ def tile_list_bonsai_vigour_page_kernel(
         warm_out = held([P, 1], F32, "warm_out")
         nc.vector.memset(tabs[:, :T].bitcast(I32), 0)
         nc.gpsimd.memset(tabs[:, T:].bitcast(I32), 0)
-        nc.gpsimd.memset(wds_raw[:].bitcast(I32), 0)
+        nc.vector.memset(wds_raw[:].bitcast(I32), 0)
         nc.vector.memset(warm_in[:], 0.0)
         nc.scalar.activation(out=warm_out[:], in_=warm_in[:], func=ACT.Exp)
 
@@ -77,17 +77,8 @@ def tile_list_bonsai_vigour_page_kernel(
         def load_show(n):
             nc.sync.dma_start(out=shw[n][:], in_=show_rows[n // 4, n % 4])
 
-        for q in range(4):
-            nc.gpsimd.dma_start(
-                out=wds_raw[32 * q : 32 * q + 4, :].bitcast(I32).rearrange("r (a c) -> r a c", a=2),
-                in_=wd_sc32[:, 4 * q : 4 * q + 4, :].rearrange("a r c -> r a c"),
-            )
 
         nc.sync.dma_start(o1[:], offs)
-        nc.sync.dma_start(o2[:], offs2)
-        nc.sync.dma_start(o3[:], offs3)
-        nc.sync.dma_start(out=low_t[:], in_=low.rearrange("(b p t) -> p b t", b=2, t=4))
-        nc.sync.dma_start(out=vec_t[:], in_=vec.rearrange("(b p t) -> p b t", b=2, t=4))
         nc.sync.dma_start(
             out=wdw_raw[:].bitcast(I32).rearrange("p (a c) -> p a c", a=2),
             in_=wd_words.bitcast(I32).rearrange("a p c -> p a c"),
@@ -99,12 +90,21 @@ def tile_list_bonsai_vigour_page_kernel(
                 in_=tab_sc32[:, 4 * q : 4 * q + 4, :].rearrange("a r c -> r a c"),
             )
         load_tabw(1)
+        for q in range(4):
+            nc.sync.dma_start(
+                out=wds_raw[32 * q : 32 * q + 4, :].bitcast(I32).rearrange("r (a c) -> r a c", a=2),
+                in_=wd_sc32[:, 4 * q : 4 * q + 4, :].rearrange("a r c -> r a c"),
+            )
         load_w1(0, 0)
         load_w1(1, 0)
         load_page(0)
+        nc.sync.dma_start(o2[:], offs2)
         for q in (0, 2, 1, 3):
             nc.sync.dma_start(out=gain0[32 * q : 32 * q + 32, :], in_=wgs_rows[:, 0, :])
         load_show(0)
+        nc.sync.dma_start(o3[:], offs3)
+        nc.sync.dma_start(out=low_t[:], in_=low.rearrange("(b p t) -> p b t", b=2, t=4))
+        nc.sync.dma_start(out=vec_t[:], in_=vec.rearrange("(b p t) -> p b t", b=2, t=4))
         for q in (0, 2, 1, 3):
             nc.sync.dma_start(out=gain123[32 * q : 32 * q + 32, :, :], in_=wgs_rows[:, 1:4, :])
         load_page(1)
@@ -122,19 +122,25 @@ def tile_list_bonsai_vigour_page_kernel(
         vw = [held([P, S], U32, "vw%d" % a) for a in range(2)]
         vs = [held([P, S], U8, "vs%d" % a) for a in range(2)]
         wdw = held([P, 4 * H], U8, "wdw")
-        wds = held([P, 2 * H], U8, "wds", "tabw0")
+        wds = {}
+
+        def deal_wd_scales(b, t0, t1, tag):
+            dealt = held([P, 2, t1 - t0, P], U8, "wds%d%d" % (b, t0), tag)
+            src = wds_raw[:].rearrange("p (a b m t) -> p b a t m", a=2, b=2, t=4)
+            nc.vector.tensor_copy(out=dealt[:], in_=src[:, b, :, t0:t1, :])
+            for a in range(2):
+                for t in range(t0, t1):
+                    wds[a, b, t] = dealt[:, a, t - t0, :]
+
         nc.vector.tensor_copy(
             out=wdw[:].bitcast(U16).rearrange("p (g t m) -> p g t m", g=4, t=4),
             in_=wdw_raw[:].bitcast(U16).rearrange("p (g m t) -> p g t m", g=4, t=4),
         )
         nc.vector.tensor_copy(vw[0][:], tabw[0][:].indirect(o1[:]))
         nc.vector.tensor_copy(vs[0][:], tabs[:, :T].indirect(o1[:]))
-        nc.vector.tensor_copy(
-            out=wds[:].rearrange("p (g t m) -> p g t m", g=4, t=4),
-            in_=wds_raw[:].rearrange("p (g m t) -> p g t m", g=4, t=4),
-        )
         nc.vector.tensor_copy(vs[1][:], tabs[:, T:].indirect(o1[:]))
         nc.vector.tensor_copy(vw[1][:], tabw[1][:].indirect(o1[:]))
+        deal_wd_scales(0, 0, 1, "tabw1")
 
         w1c = {}
         w1s = {}
@@ -143,8 +149,12 @@ def tile_list_bonsai_vigour_page_kernel(
             nt = t1 - t0
             name = "%d%d%d" % (a, b, t0)
             stage = held([P, nt * 512], BF16, "w1bf" + name, tag)
-            src = w1raw[a, b][:].rearrange("p j (m t) -> p m j t", t=4)[:, :, :, t0:t1]
-            dst = stage[:].rearrange("p (t m j) -> p m j t", t=nt, j=4)
+            if nt == 1:
+                src = w1raw[a, b][:].rearrange("p j (m t) -> p t m j", t=4)[:, t0, :, :]
+                dst = stage[:].rearrange("p (m j) -> p m j", j=4)
+            else:
+                src = w1raw[a, b][:].rearrange("p j (m e t) -> p m j e t", e=2, t=4)[:, :, :, :, t0:t1]
+                dst = stage[:].rearrange("p (t m e j) -> p m j e t", t=nt, e=2, j=4)
             if engine == "scalar":
                 nc.scalar.copy(out=dst, in_=src)
             else:
@@ -177,7 +187,7 @@ def tile_list_bonsai_vigour_page_kernel(
                 nc.tensor.matmul_mx(
                     out=second[:],
                     lhsT=wdw[:, 256 * g : 256 * (g + 1)].bitcast(FP4X4),
-                    lhsT_scale=wds[:, P * g : P * (g + 1)],
+                    lhsT_scale=wds[a, b, t],
                     rhs=vw[a][:].bitcast(FP8X4),
                     rhs_scale=vs[a][:],
                     start=(a == 0),
@@ -200,16 +210,19 @@ def tile_list_bonsai_vigour_page_kernel(
             sq[n] = ring.tile([P, S], F32, name="sq%d" % n, tag="sq", bufs=4, align_bytes=64)
             nc.scalar.activation(out=sq[n][:], in_=first[:], func=ACT.Square)
 
-        h_tags = ["hA", "hB", "hA", "hB", "hA", "hB", "pgbf0", "xil0"]
-
         def sub(n):
-            hh[n] = held([P, S], F32, "h%d" % n, h_tags[n])
-            nc.vector.tensor_tensor(out=hh[n][:], in0=sq[n][:], in1=banks[n][:], op=ALU.subtract)
+            if n < 3:
+                hh[n] = held([P, S], F32, "h%d" % n, "hB" if n < 2 else None)[:]
+            else:
+                pair = held([P, 2, S], F32, "hy%d" % n, "page%d" % (n - 3))
+                hh[n] = pair[:, 0, :]
+                yy[n - 1] = pair[:, 1, :]
+            nc.vector.tensor_tensor(out=hh[n], in0=sq[n][:], in1=banks[n][:], op=ALU.subtract)
 
         def scatter(n):
             t = n % 4
             gain = gain0[:] if t == 0 else gain123[:, t - 1, :]
-            nc.vector.tensor_tensor(page[n][:].indirect(o2[:]), hh[n][:], gain, ALU.mult)
+            nc.vector.tensor_tensor(page[n][:].indirect(o2[:]), hh[n], gain, ALU.mult)
 
         pgbf = [held([P, 4 * T2], BF16, "pgbf%d" % b) for b in range(2)]
 
@@ -230,8 +243,9 @@ def tile_list_bonsai_vigour_page_kernel(
                 pscales[b, c] = scales[:, c * P - c0 : (c + 1) * P - c0]
 
         def gather(n):
-            yy[n] = ring.tile([P, PJ], F32, name="y%d" % n, tag="y", align_bytes=64)
-            nc.vector.tensor_tensor(yy[n][:], page[n][:].indirect(o3[:]), shw[n][:], ALU.mult)
+            if n not in yy:
+                yy[n] = held([P, PJ], F32, "y%d" % n, "hA" if n == 0 else None)[:]
+            nc.vector.tensor_tensor(yy[n], page[n][:].indirect(o3[:]), shw[n][:], ALU.mult)
 
         xst = [held([P, 4, PJ], BF16, "xst%d" % b) for b in range(2)]
         xil = [held([P, 4 * PJ], BF16, "xil%d" % b) for b in range(2)]
@@ -240,22 +254,20 @@ def tile_list_bonsai_vigour_page_kernel(
 
         def floor_scale(n):
             b, t = divmod(n, 4)
+            woven = xil[b][:].rearrange("p (j t) -> p t j", t=4)
             nc.vector.tensor_scalar(
-                out=xst[b][:, t, :],
-                in0=yy[n][:],
+                out=xst[b][:, t, :] if n < 6 else woven[:, t, :],
+                in0=yy[n],
                 scalar1=low_t[:, b, t : t + 1],
                 scalar2=vec_t[:, b, t : t + 1],
                 op0=ALU.max,
                 op1=ALU.mult,
             )
 
-        def x_weave(b, engine):
+        def x_weave(b, planes):
             dst = xil[b][:].rearrange("p (c i t) -> p c t i", i=4, t=4)
             src = xst[b][:].rearrange("p t (c i) -> p c t i", i=4)
-            if engine == "scalar":
-                nc.scalar.copy(out=dst, in_=src)
-            else:
-                nc.vector.tensor_copy(out=dst, in_=src)
+            nc.scalar.copy(out=dst[:, :, :planes, :], in_=src[:, :, :planes, :])
 
         def x_quant(b):
             nc.vector.quantize_mx(out=xc[b][:].bitcast(FP8X4), scales=xs[b][:], in_=xil[b][:])
@@ -275,50 +287,53 @@ def tile_list_bonsai_vigour_page_kernel(
                 stop=(b == 1),
             )
 
-        def epilogue(c):
-            mn = ring.tile([P, PJ], F32, name="mn%d" % c, tag="y", align_bytes=64)
+        def epilogue(c, j0, j1):
+            mn = ring.tile([P, j1 - j0], F32, name="mn%d_%d" % (c, j0), tag="y", align_bytes=64)
             nc.vector.tensor_scalar(
-                out=mn[:], in0=ebank[c][:], scalar1=slot_t[:, c : c + 1], scalar2=None, op0=ALU.min
+                out=mn[:], in0=ebank[c][:, j0:j1], scalar1=slot_t[:, c : c + 1], scalar2=None, op0=ALU.min
             )
-            ex = ring.tile([P, PJ], F32, name="ex%d" % c, tag="sq", bufs=4, align_bytes=64)
+            ex = held([P, j1 - j0], F32, "ex%d_%d" % (c, j0), "show%d" % c if j0 == 0 else "gain0")
             nc.scalar.activation(out=ex[:], in_=mn[:], func=ACT.Exp)
-            nc.sync.dma_start(out=out[c * P : (c + 1) * P, :], in_=ex[:])
+            nc.sync.dma_start(out=out[c * P : (c + 1) * P, j0:j1], in_=ex[:])
 
-        for n in range(4):
-            second_product(n, (0,))
-        second_product(0, (1,))
+        second_product(0)
         q00a = w1_piece(0, 0, 0, 1, "scalar")
         q00b = w1_piece(0, 0, 1, 4, "scalar")
         q00a(0, 1)
-        q10a = w1_piece(1, 0, 0, 1, "vector", "wds_raw")
+        q10a = w1_piece(1, 0, 0, 1, "vector", "tabs")
         q10a(0, 1)
         first_product(0)
-        q10b = w1_piece(1, 0, 1, 4, "vector")
+        deal_wd_scales(0, 1, 4, "tabs")
+        q10b = w1_piece(1, 0, 1, 2, "vector")
         q00b(1, 2)
         q10b(1, 2)
-        second_product(1, (1,))
+        second_product(1)
         first_product(1)
+        q10c = w1_piece(1, 0, 2, 4, "scalar")
         sub(0)
-        later = {}
         for n in range(8):
             scatter(n)
+            if n > 0:
+                floor_scale(n - 1)
             if n == 0:
                 q00b(2, 4)
-                q10b(2, 4)
+                q10c(2, 4)
+                deal_wd_scales(1, 0, 4, "w1bf101")
                 for m in (2, 3):
-                    second_product(m, (1,))
+                    second_product(m)
                     first_product(m)
-            if n < 2:
-                later[n] = w1_piece(n, 1, 0, 4, "scalar", h_tags[n])
-            if n in (1, 2):
-                later[n - 1](0, 4)
-            if 2 <= n < 6:
-                second_product(n + 2)
-                first_product(n + 2)
+            if n == 1:
+                for a in range(2):
+                    w1_piece(a, 1, 0, 4, "scalar", "hA" if a == 0 else "hB")(0, 4)
+                for m in range(4, 8):
+                    second_product(m)
+                    first_product(m)
             if n == 4:
+                x_weave(0, 4)
                 page_quant(0, 0, T2)
-            if n == 5:
                 x_quant(0)
+            if n == 6:
+                x_weave(1, 2)
             if n + 1 < 8:
                 sub(n + 1)
             if n < 7:
@@ -327,19 +342,18 @@ def tile_list_bonsai_vigour_page_kernel(
                 for c in range(4):
                     page_round(n, 256 * c, 256 * (c + 1))
             gather(n)
-            if n > 0:
-                floor_scale(n - 1)
-            if n == 4:
-                x_weave(0, "scalar")
         for c in range(8):
             final_pass(0, c)
         page_quant(1, 0, 256)
         floor_scale(7)
         page_quant(1, 256, 512)
-        x_weave(1, "vector")
-        page_quant(1, 512, 768)
         x_quant(1)
+        page_quant(1, 512, 768)
         page_quant(1, 768, 1024)
         for c in range(8):
             final_pass(1, c)
-            epilogue(c)
+            if c < 7:
+                epilogue(c, 0, PJ)
+            else:
+                epilogue(c, 0, PJ // 2)
+                epilogue(c, PJ // 2, PJ)

@@ -84,18 +84,18 @@ def tile_list_bonsai_vigour_page_kernel(
             in_=wd_words.bitcast(I32).rearrange("a p c -> p a c"),
         )
         load_tabw(0)
-        for q in range(4):
+        for r in range(4):
             nc.sync.dma_start(
-                out=tabs[32 * q : 32 * q + 4, :].bitcast(I32).rearrange("r (a c) -> r a c", a=2),
-                in_=tab_sc32[:, 4 * q : 4 * q + 4, :].rearrange("a r c -> r a c"),
+                out=tabs[r:P:32, :].bitcast(I32).rearrange("q (a c) -> q a c", a=2),
+                in_=tab_sc32.rearrange("a (q r) c -> r q a c", r=4)[r],
             )
         load_tabw(1)
-        for q in range(4):
-            nc.sync.dma_start(
-                out=wds_raw[32 * q : 32 * q + 4, :].bitcast(I32).rearrange("r (a c) -> r a c", a=2),
-                in_=wd_sc32[:, 4 * q : 4 * q + 4, :].rearrange("a r c -> r a c"),
-            )
         load_w1(0, 0)
+        for r in range(4):
+            nc.sync.dma_start(
+                out=wds_raw[r:P:32, :].bitcast(I32).rearrange("q (a c) -> q a c", a=2),
+                in_=wd_sc32.rearrange("a (q r) c -> r q a c", r=4)[r],
+            )
         load_w1(1, 0)
         load_page(0)
         nc.sync.dma_start(o2[:], offs2)
@@ -141,6 +141,7 @@ def tile_list_bonsai_vigour_page_kernel(
         nc.vector.tensor_copy(vs[1][:], tabs[:, T:].indirect(o1[:]))
         nc.vector.tensor_copy(vw[1][:], tabw[1][:].indirect(o1[:]))
         deal_wd_scales(0, 0, 1, "tabw1")
+        deal_wd_scales(1, 0, 4, "tabw0")
 
         w1c = {}
         w1s = {}
@@ -160,8 +161,8 @@ def tile_list_bonsai_vigour_page_kernel(
             else:
                 nc.vector.tensor_copy(out=dst, in_=src)
 
-            def quant(c0, c1):
-                codes = held([P, (c1 - c0) * P], U32, "w1c%s%d" % (name, c0))
+            def quant(c0, c1, codes_tag=None):
+                codes = held([P, (c1 - c0) * P], U32, "w1c%s%d" % (name, c0), codes_tag)
                 scales = held([P, (c1 - c0) * P], U8, "w1s%s%d" % (name, c0))
                 nc.vector.quantize_mx(
                     out=codes[:].bitcast(FP8X4), scales=scales[:], in_=stage[:, (c0 - t0) * 512 : (c1 - t0) * 512]
@@ -212,7 +213,7 @@ def tile_list_bonsai_vigour_page_kernel(
 
         def sub(n):
             if n < 3:
-                hh[n] = held([P, S], F32, "h%d" % n, "hB" if n < 2 else None)[:]
+                hh[n] = held([P, S], F32, "h%d" % n, "hB" if n < 2 else "show0")[:]
             else:
                 pair = held([P, 2, S], F32, "hy%d" % n, "page%d" % (n - 3))
                 hh[n] = pair[:, 0, :]
@@ -305,7 +306,7 @@ def tile_list_bonsai_vigour_page_kernel(
         first_product(0)
         deal_wd_scales(0, 1, 4, "tabs")
         q10b = w1_piece(1, 0, 1, 2, "vector")
-        q00b(1, 2)
+        q00b(1, 2, "w1c1000")
         q10b(1, 2)
         second_product(1)
         first_product(1)
@@ -316,9 +317,8 @@ def tile_list_bonsai_vigour_page_kernel(
             if n > 0:
                 floor_scale(n - 1)
             if n == 0:
-                q00b(2, 4)
+                q00b(2, 4, "w1s1000")
                 q10c(2, 4)
-                deal_wd_scales(1, 0, 4, "w1bf101")
                 for m in (2, 3):
                     second_product(m)
                     first_product(m)

@@ -2,7 +2,7 @@ from contextlib import ExitStack
 
 import concourse.mybir as mybir
 
-K, H, T, S, T2, PJ = 1024, 1024, 2048, 512, 1024, 512
+H, T, S, T2, PJ = 1024, 2048, 512, 1024, 512
 FLOPS = 3221225472
 
 F32 = mybir.dt.float32
@@ -17,6 +17,17 @@ ALU = mybir.AluOpType
 ACT = mybir.ActivationFunctionType
 
 P = 128
+PACK = 4
+SPAN = P * PACK
+PASSES = 2
+ROW_TILES = PASSES * PACK
+LAST = ROW_TILES - 1
+OUT_TILES = T2 // P
+QUADRANT = 32
+QUADRANT_ORDER = (0, 2, 1, 3)
+SQUARES_AHEAD = 4
+PAGE_LAG = 3
+TAIL_CHUNK = 256
 
 
 def tile_list_bonsai_vigour_page_kernel(
@@ -32,328 +43,326 @@ def tile_list_bonsai_vigour_page_kernel(
         def held(shape, dtype, name, tag=None):
             return keep.tile(shape, dtype, name=name, tag=tag or name, align_bytes=64)
 
-        o1 = lists.tile([P, S // 16], U16, name="o1")
-        o2 = lists.tile([P, S // 16], U16, name="o2")
-        o3 = lists.tile([P, PJ // 16], U16, name="o3")
-        wds_raw = held([P, 2 * H], U8, "wds_raw")
-        tabs = held([P, 2 * T], U8, "tabs")
-        warm_in = held([P, 1], F32, "warm_in")
-        warm_out = held([P, 1], F32, "warm_out")
-        nc.vector.memset(tabs[:, :T].bitcast(I32), 0)
-        nc.gpsimd.memset(tabs[:, T:].bitcast(I32), 0)
-        nc.vector.memset(wds_raw[:].bitcast(I32), 0)
-        nc.vector.memset(warm_in[:], 0.0)
-        nc.scalar.activation(out=warm_out[:], in_=warm_in[:], func=ACT.Exp)
+        scan_list = lists.tile([P, S // 16], U16, name="o1")
+        slot_list = lists.tile([P, S // 16], U16, name="o2")
+        show_list = lists.tile([P, PJ // 16], U16, name="o3")
 
-        tabw = [held([P, T], U32, "tabw%d" % a) for a in range(2)]
-        w1raw = {(a, b): held([P, 4, 512], F32, "w1raw%d%d" % (a, b)) for a in range(2) for b in range(2)}
-        wdw_raw = held([P, 4 * H], U8, "wdw_raw")
-        page = [held([P, T2], F32, "page%d" % n) for n in range(8)]
-        shw = [held([P, PJ], F32, "show%d" % n) for n in range(8)]
-        gain0 = held([P, S], F32, "gain0")
-        gain123 = held([P, 3, S], F32, "gain123")
-        low_t = held([P, 2, 4], F32, "low_t")
-        vec_t = held([P, 2, 4], F32, "vec_t")
-        slot_t = held([P, 8], F32, "slot_t")
+        wd_scale_rows = held([P, PASSES * H], U8, "wds_raw")
+        tab_scale_rows = held([P, PASSES * T], U8, "tabs")
+        nc.vector.memset(tab_scale_rows[:, :T].bitcast(I32), 0)
+        nc.gpsimd.memset(tab_scale_rows[:, T:].bitcast(I32), 0)
+        nc.vector.memset(wd_scale_rows[:].bitcast(I32), 0)
 
-        page_rows = page0.rearrange("(b p t) m -> b t p m", b=2, t=4)
-        show_rows = show.rearrange("(b p t) j -> b t p j", b=2, t=4)
-        wgs_rows = wgs.rearrange("(p t) j -> p t j", t=4)
-        tab_sc32 = tab_scales.bitcast(I32)
-        wd_sc32 = wd_scales.bitcast(I32)
+        tab_word_rows = [held([P, T], U32, "tabw%d" % a) for a in range(PASSES)]
+        w1_rows = {
+            (a, b): held([P, PACK, SPAN], F32, "w1raw%d%d" % (a, b)) for a in range(PASSES) for b in range(PASSES)
+        }
+        wd_word_rows = held([P, PASSES * 2 * H], U8, "wdw_raw")
+        page = [held([P, T2], F32, "page%d" % n) for n in range(ROW_TILES)]
+        show_tile = [held([P, PJ], F32, "show%d" % n) for n in range(ROW_TILES)]
+        gain_first = held([P, S], F32, "gain0")
+        gain_rest = held([P, PACK - 1, S], F32, "gain123")
+        low_cols = held([P, PASSES, PACK], F32, "low_t")
+        vec_cols = held([P, PASSES, PACK], F32, "vec_t")
+        slot_cols = held([P, OUT_TILES], F32, "slot_t")
 
-        def load_tabw(a):
-            nc.sync.dma_start(out=tabw[a][:].bitcast(I32), in_=tab_words[a].rearrange("p n t -> p (n t)").bitcast(I32))
+        page_rows = page0.rearrange("(b p t) m -> b t p m", b=PASSES, t=PACK)
+        show_rows = show.rearrange("(b p t) j -> b t p j", b=PASSES, t=PACK)
+        wgs_rows = wgs.rearrange("(p t) j -> p t j", t=PACK)
+
+        def load_tab_words(a):
+            nc.sync.dma_start(
+                out=tab_word_rows[a][:].bitcast(I32), in_=tab_words[a].rearrange("p n t -> p (n t)").bitcast(I32)
+            )
+
+        def load_scale_rows(tile, scales):
+            for i in range(PACK):
+                nc.sync.dma_start(
+                    out=tile[i:P:QUADRANT, :].bitcast(I32).rearrange("q (a c) -> q a c", a=PASSES),
+                    in_=scales.bitcast(I32).rearrange("a (q i) c -> i q a c", i=PACK)[i],
+                )
 
         def load_w1(a, b):
             nc.sync.dma_start(
-                out=w1raw[a, b][:],
-                in_=w1[512 * a : 512 * (a + 1), 512 * b : 512 * (b + 1)].rearrange("(p j) c -> p j c", j=4),
+                out=w1_rows[a, b][:],
+                in_=w1[SPAN * a : SPAN * (a + 1), SPAN * b : SPAN * (b + 1)].rearrange("(p i) c -> p i c", i=PACK),
             )
 
         def load_page(n):
-            nc.sync.dma_start(out=page[n][:], in_=page_rows[n // 4, n % 4])
+            nc.sync.dma_start(out=page[n][:], in_=page_rows[n // PACK, n % PACK])
 
         def load_show(n):
-            nc.sync.dma_start(out=shw[n][:], in_=show_rows[n // 4, n % 4])
+            nc.sync.dma_start(out=show_tile[n][:], in_=show_rows[n // PACK, n % PACK])
 
-
-        nc.sync.dma_start(o1[:], offs)
+        nc.sync.dma_start(scan_list[:], offs)
         nc.sync.dma_start(
-            out=wdw_raw[:].bitcast(I32).rearrange("p (a c) -> p a c", a=2),
+            out=wd_word_rows[:].bitcast(I32).rearrange("p (a c) -> p a c", a=PASSES),
             in_=wd_words.bitcast(I32).rearrange("a p c -> p a c"),
         )
-        load_tabw(0)
-        for r in range(4):
-            nc.sync.dma_start(
-                out=tabs[r:P:32, :].bitcast(I32).rearrange("q (a c) -> q a c", a=2),
-                in_=tab_sc32.rearrange("a (q r) c -> r q a c", r=4)[r],
-            )
-        load_tabw(1)
+        load_tab_words(0)
+        load_scale_rows(tab_scale_rows, tab_scales)
+        load_tab_words(1)
         load_w1(0, 0)
-        for r in range(4):
-            nc.sync.dma_start(
-                out=wds_raw[r:P:32, :].bitcast(I32).rearrange("q (a c) -> q a c", a=2),
-                in_=wd_sc32.rearrange("a (q r) c -> r q a c", r=4)[r],
-            )
+        load_scale_rows(wd_scale_rows, wd_scales)
         load_w1(1, 0)
         load_page(0)
-        nc.sync.dma_start(o2[:], offs2)
-        for q in (0, 2, 1, 3):
-            nc.sync.dma_start(out=gain0[32 * q : 32 * q + 32, :], in_=wgs_rows[:, 0, :])
+        nc.sync.dma_start(slot_list[:], offs2)
+        for q in QUADRANT_ORDER:
+            nc.sync.dma_start(out=gain_first[QUADRANT * q : QUADRANT * (q + 1), :], in_=wgs_rows[:, 0, :])
         load_show(0)
-        nc.sync.dma_start(o3[:], offs3)
-        nc.sync.dma_start(out=low_t[:], in_=low.rearrange("(b p t) -> p b t", b=2, t=4))
-        nc.sync.dma_start(out=vec_t[:], in_=vec.rearrange("(b p t) -> p b t", b=2, t=4))
-        for q in (0, 2, 1, 3):
-            nc.sync.dma_start(out=gain123[32 * q : 32 * q + 32, :, :], in_=wgs_rows[:, 1:4, :])
+        nc.sync.dma_start(show_list[:], offs3)
+        nc.sync.dma_start(out=low_cols[:], in_=low.rearrange("(b p t) -> p b t", b=PASSES, t=PACK))
+        nc.sync.dma_start(out=vec_cols[:], in_=vec.rearrange("(b p t) -> p b t", b=PASSES, t=PACK))
+        for q in QUADRANT_ORDER:
+            nc.sync.dma_start(out=gain_rest[QUADRANT * q : QUADRANT * (q + 1), :, :], in_=wgs_rows[:, 1:PACK, :])
         load_page(1)
         load_w1(0, 1)
         load_show(1)
         load_page(2)
         load_w1(1, 1)
         load_show(2)
-        for n in range(3, 8):
+        for n in range(3, ROW_TILES):
             load_page(n)
             load_show(n)
         with nc.allow_non_contiguous_dma(reason="one value a partition"):
-            nc.sync.dma_start(out=slot_t[:], in_=slot.rearrange("(c p) -> p c", p=P))
+            nc.sync.dma_start(out=slot_cols[:], in_=slot.rearrange("(c p) -> p c", p=P))
 
-        vw = [held([P, S], U32, "vw%d" % a) for a in range(2)]
-        vs = [held([P, S], U8, "vs%d" % a) for a in range(2)]
-        wdw = held([P, 4 * H], U8, "wdw")
-        wds = {}
+        v_words = [held([P, S], U32, "vw%d" % a) for a in range(PASSES)]
+        v_scales = [held([P, S], U8, "vs%d" % a) for a in range(PASSES)]
+        wd_dealt_words = held([P, PASSES * 2 * H], U8, "wdw")
+        wd_dealt_scales = {}
 
         def deal_wd_scales(b, t0, t1, tag):
-            dealt = held([P, 2, t1 - t0, P], U8, "wds%d%d" % (b, t0), tag)
-            src = wds_raw[:].rearrange("p (a b m t) -> p b a t m", a=2, b=2, t=4)
+            dealt = held([P, PASSES, t1 - t0, P], U8, "wds%d%d" % (b, t0), tag)
+            src = wd_scale_rows[:].rearrange("p (a b m t) -> p b a t m", a=PASSES, b=PASSES, t=PACK)
             nc.vector.tensor_copy(out=dealt[:], in_=src[:, b, :, t0:t1, :])
-            for a in range(2):
+            for a in range(PASSES):
                 for t in range(t0, t1):
-                    wds[a, b, t] = dealt[:, a, t - t0, :]
+                    wd_dealt_scales[a, b, t] = dealt[:, a, t - t0, :]
 
         nc.vector.tensor_copy(
-            out=wdw[:].bitcast(U16).rearrange("p (g t m) -> p g t m", g=4, t=4),
-            in_=wdw_raw[:].bitcast(U16).rearrange("p (g m t) -> p g t m", g=4, t=4),
+            out=wd_dealt_words[:].bitcast(U16).rearrange("p (g t m) -> p g t m", g=PASSES * PASSES, t=PACK),
+            in_=wd_word_rows[:].bitcast(U16).rearrange("p (g m t) -> p g t m", g=PASSES * PASSES, t=PACK),
         )
-        nc.vector.tensor_copy(vw[0][:], tabw[0][:].indirect(o1[:]))
-        nc.vector.tensor_copy(vs[0][:], tabs[:, :T].indirect(o1[:]))
-        nc.vector.tensor_copy(vs[1][:], tabs[:, T:].indirect(o1[:]))
-        nc.vector.tensor_copy(vw[1][:], tabw[1][:].indirect(o1[:]))
+        nc.vector.tensor_copy(v_words[0][:], tab_word_rows[0][:].indirect(scan_list[:]))
+        nc.vector.tensor_copy(v_scales[0][:], tab_scale_rows[:, :T].indirect(scan_list[:]))
+        nc.vector.tensor_copy(v_scales[1][:], tab_scale_rows[:, T:].indirect(scan_list[:]))
+        nc.vector.tensor_copy(v_words[1][:], tab_word_rows[1][:].indirect(scan_list[:]))
         deal_wd_scales(0, 0, 1, "tabw1")
-        deal_wd_scales(1, 0, 4, "tabw0")
+        deal_wd_scales(1, 0, PACK, "tabw0")
 
-        w1c = {}
-        w1s = {}
+        w1_codes = {}
+        w1_scales = {}
 
-        def w1_piece(a, b, t0, t1, engine, tag=None):
-            nt = t1 - t0
+        def weave_w1(a, b, t0, t1, copy, tag=None):
+            count = t1 - t0
             name = "%d%d%d" % (a, b, t0)
-            stage = held([P, nt * 512], BF16, "w1bf" + name, tag)
-            if nt == 1:
-                src = w1raw[a, b][:].rearrange("p j (m t) -> p t m j", t=4)[:, t0, :, :]
-                dst = stage[:].rearrange("p (m j) -> p m j", j=4)
+            woven = held([P, count * SPAN], BF16, "w1bf" + name, tag)
+            if count == 1:
+                src = w1_rows[a, b][:].rearrange("p i (m t) -> p t m i", t=PACK)[:, t0, :, :]
+                dst = woven[:].rearrange("p (m i) -> p m i", i=PACK)
             else:
-                src = w1raw[a, b][:].rearrange("p j (m e t) -> p m j e t", e=2, t=4)[:, :, :, :, t0:t1]
-                dst = stage[:].rearrange("p (t m e j) -> p m j e t", t=nt, e=2, j=4)
-            if engine == "scalar":
-                nc.scalar.copy(out=dst, in_=src)
-            else:
-                nc.vector.tensor_copy(out=dst, in_=src)
+                src = w1_rows[a, b][:].rearrange("p i (m e t) -> p m i e t", e=2, t=PACK)[:, :, :, :, t0:t1]
+                dst = woven[:].rearrange("p (t m e i) -> p m i e t", t=count, e=2, i=PACK)
+            copy(out=dst, in_=src)
 
-            def quant(c0, c1, codes_tag=None):
-                codes = held([P, (c1 - c0) * P], U32, "w1c%s%d" % (name, c0), codes_tag)
-                scales = held([P, (c1 - c0) * P], U8, "w1s%s%d" % (name, c0))
+            def quantise(u0, u1, codes_tag=None):
+                codes = held([P, (u1 - u0) * P], U32, "w1c%s%d" % (name, u0), codes_tag)
+                scales = held([P, (u1 - u0) * P], U8, "w1s%s%d" % (name, u0))
                 nc.vector.quantize_mx(
-                    out=codes[:].bitcast(FP8X4), scales=scales[:], in_=stage[:, (c0 - t0) * 512 : (c1 - t0) * 512]
+                    out=codes[:].bitcast(FP8X4), scales=scales[:], in_=woven[:, (u0 - t0) * SPAN : (u1 - t0) * SPAN]
                 )
-                for t in range(c0, c1):
-                    w1c[a, b, t] = codes[:, (t - c0) * P : (t - c0 + 1) * P]
-                    w1s[a, b, t] = scales[:, (t - c0) * P : (t - c0 + 1) * P]
+                for t in range(u0, u1):
+                    w1_codes[a, b, t] = codes[:, (t - u0) * P : (t - u0 + 1) * P]
+                    w1_scales[a, b, t] = scales[:, (t - u0) * P : (t - u0 + 1) * P]
 
-            return quant
+            return quantise
 
-        banks = {}
-        sq = {}
-        hh = {}
-        yy = {}
+        second = {}
+        squared = {}
+        h = {}
+        picked = {}
 
-        def second_product(n, passes=(0, 1)):
-            b, t = divmod(n, 4)
-            if n not in banks:
-                banks[n] = psum.tile([P, S], F32, name="second%d" % n, tag="bank%d" % ((2 * n + 1) % 8))
-            second = banks[n]
-            for a in passes:
-                g = (2 * a + b) * 4 + t
+        def second_product(n):
+            b, t = divmod(n, PACK)
+            second[n] = psum.tile([P, S], F32, name="second%d" % n, tag="bank%d" % (2 * (n % SQUARES_AHEAD) + 1))
+            for a in range(PASSES):
+                byte0 = 2 * P * ((PASSES * a + b) * PACK + t)
                 nc.tensor.matmul_mx(
-                    out=second[:],
-                    lhsT=wdw[:, 256 * g : 256 * (g + 1)].bitcast(FP4X4),
-                    lhsT_scale=wds[a, b, t],
-                    rhs=vw[a][:].bitcast(FP8X4),
-                    rhs_scale=vs[a][:],
+                    out=second[n][:],
+                    lhsT=wd_dealt_words[:, byte0 : byte0 + 2 * P].bitcast(FP4X4),
+                    lhsT_scale=wd_dealt_scales[a, b, t],
+                    rhs=v_words[a][:].bitcast(FP8X4),
+                    rhs_scale=v_scales[a][:],
                     start=(a == 0),
-                    stop=(a == 1),
+                    stop=(a == PASSES - 1),
                 )
 
-        def first_product(n):
-            b, t = divmod(n, 4)
-            first = psum.tile([P, S], F32, name="first%d" % n, tag="bank%d" % (2 * n % 8))
-            for a in range(2):
+        def first_product_squared(n):
+            b, t = divmod(n, PACK)
+            first = psum.tile([P, S], F32, name="first%d" % n, tag="bank%d" % (2 * (n % SQUARES_AHEAD)))
+            for a in range(PASSES):
                 nc.tensor.matmul_mx(
                     out=first[:],
-                    lhsT=w1c[a, b, t].bitcast(FP8X4),
-                    lhsT_scale=w1s[a, b, t],
-                    rhs=vw[a][:].bitcast(FP8X4),
-                    rhs_scale=vs[a][:],
+                    lhsT=w1_codes[a, b, t].bitcast(FP8X4),
+                    lhsT_scale=w1_scales[a, b, t],
+                    rhs=v_words[a][:].bitcast(FP8X4),
+                    rhs_scale=v_scales[a][:],
                     start=(a == 0),
-                    stop=(a == 1),
+                    stop=(a == PASSES - 1),
                 )
-            sq[n] = ring.tile([P, S], F32, name="sq%d" % n, tag="sq", bufs=4, align_bytes=64)
-            nc.scalar.activation(out=sq[n][:], in_=first[:], func=ACT.Square)
+            squared[n] = ring.tile([P, S], F32, name="sq%d" % n, tag="sq", bufs=SQUARES_AHEAD, align_bytes=64)
+            nc.scalar.activation(out=squared[n][:], in_=first[:], func=ACT.Square)
 
-        def sub(n):
-            if n < 3:
-                hh[n] = held([P, S], F32, "h%d" % n, "hB" if n < 2 else "show0")[:]
+        early_h_tags = ("hB", "hB", "show0")
+
+        def subtract(n):
+            if n < PAGE_LAG:
+                h[n] = held([P, S], F32, "h%d" % n, early_h_tags[n])[:]
             else:
-                pair = held([P, 2, S], F32, "hy%d" % n, "page%d" % (n - 3))
-                hh[n] = pair[:, 0, :]
-                yy[n - 1] = pair[:, 1, :]
-            nc.vector.tensor_tensor(out=hh[n], in0=sq[n][:], in1=banks[n][:], op=ALU.subtract)
+                pair = held([P, 2, S], F32, "hy%d" % n, "page%d" % (n - PAGE_LAG))
+                h[n] = pair[:, 0, :]
+                picked[n - 1] = pair[:, 1, :]
+            nc.vector.tensor_tensor(out=h[n], in0=squared[n][:], in1=second[n][:], op=ALU.subtract)
 
         def scatter(n):
-            t = n % 4
-            gain = gain0[:] if t == 0 else gain123[:, t - 1, :]
-            nc.vector.tensor_tensor(page[n][:].indirect(o2[:]), hh[n], gain, ALU.mult)
+            t = n % PACK
+            gain = gain_first[:] if t == 0 else gain_rest[:, t - 1, :]
+            nc.vector.tensor_tensor(page[n][:].indirect(slot_list[:]), h[n], gain, ALU.mult)
 
-        pgbf = [held([P, 4 * T2], BF16, "pgbf%d" % b) for b in range(2)]
+        page_woven = [held([P, PACK * T2], BF16, "pgbf%d" % b) for b in range(PASSES)]
 
-        def page_round(n, c0, c1):
-            b, t = divmod(n, 4)
-            dst = pgbf[b][:].rearrange("p (m t) -> p t m", t=4)
-            nc.scalar.copy(out=dst[:, t, c0:c1], in_=page[n][:, c0:c1])
+        def weave_page(n, m0, m1):
+            b, t = divmod(n, PACK)
+            dst = page_woven[b][:].rearrange("p (m t) -> p t m", t=PACK)
+            nc.scalar.copy(out=dst[:, t, m0:m1], in_=page[n][:, m0:m1])
 
-        pcodes = {}
-        pscales = {}
+        page_codes = {}
+        page_scales = {}
 
-        def page_quant(b, c0, c1):
-            codes = held([P, c1 - c0], U32, "pc%d_%d" % (b, c0))
-            scales = held([P, c1 - c0], U8, "ps%d_%d" % (b, c0))
-            nc.vector.quantize_mx(out=codes[:].bitcast(FP8X4), scales=scales[:], in_=pgbf[b][:, 4 * c0 : 4 * c1])
-            for c in range(c0 // P, c1 // P):
-                pcodes[b, c] = codes[:, c * P - c0 : (c + 1) * P - c0]
-                pscales[b, c] = scales[:, c * P - c0 : (c + 1) * P - c0]
+        def quantise_page(b, m0, m1):
+            codes = held([P, m1 - m0], U32, "pc%d_%d" % (b, m0))
+            scales = held([P, m1 - m0], U8, "ps%d_%d" % (b, m0))
+            nc.vector.quantize_mx(
+                out=codes[:].bitcast(FP8X4), scales=scales[:], in_=page_woven[b][:, PACK * m0 : PACK * m1]
+            )
+            for c in range(m0 // P, m1 // P):
+                page_codes[b, c] = codes[:, c * P - m0 : (c + 1) * P - m0]
+                page_scales[b, c] = scales[:, c * P - m0 : (c + 1) * P - m0]
 
         def gather(n):
-            if n not in yy:
-                yy[n] = held([P, PJ], F32, "y%d" % n, "hA" if n == 0 else None)[:]
-            nc.vector.tensor_tensor(yy[n], page[n][:].indirect(o3[:]), shw[n][:], ALU.mult)
+            if n not in picked:
+                picked[n] = held([P, PJ], F32, "y%d" % n, "hA" if n == 0 else None)[:]
+            nc.vector.tensor_tensor(picked[n], page[n][:].indirect(show_list[:]), show_tile[n][:], ALU.mult)
 
-        xst = [held([P, 4, PJ], BF16, "xst%d" % b) for b in range(2)]
-        xil = [held([P, 4 * PJ], BF16, "xil%d" % b) for b in range(2)]
-        xc = [held([P, PJ], U32, "xc%d" % b) for b in range(2)]
-        xs = [held([P, PJ], U8, "xs%d" % b) for b in range(2)]
+        x_rows = [held([P, PACK, PJ], BF16, "xst%d" % b) for b in range(PASSES)]
+        x_woven = [held([P, PACK * PJ], BF16, "xil%d" % b) for b in range(PASSES)]
+        x_codes = [held([P, PJ], U32, "xc%d" % b) for b in range(PASSES)]
+        x_scales = [held([P, PJ], U8, "xs%d" % b) for b in range(PASSES)]
+        first_direct = ROW_TILES - 2
 
-        def floor_scale(n):
-            b, t = divmod(n, 4)
-            woven = xil[b][:].rearrange("p (j t) -> p t j", t=4)
+        def floor_and_scale(n):
+            b, t = divmod(n, PACK)
+            places = x_woven[b][:].rearrange("p (j t) -> p t j", t=PACK)
             nc.vector.tensor_scalar(
-                out=xst[b][:, t, :] if n < 6 else woven[:, t, :],
-                in0=yy[n],
-                scalar1=low_t[:, b, t : t + 1],
-                scalar2=vec_t[:, b, t : t + 1],
+                out=x_rows[b][:, t, :] if n < first_direct else places[:, t, :],
+                in0=picked[n],
+                scalar1=low_cols[:, b, t : t + 1],
+                scalar2=vec_cols[:, b, t : t + 1],
                 op0=ALU.max,
                 op1=ALU.mult,
             )
 
-        def x_weave(b, planes):
-            dst = xil[b][:].rearrange("p (c i t) -> p c t i", i=4, t=4)
-            src = xst[b][:].rearrange("p t (c i) -> p c t i", i=4)
-            nc.scalar.copy(out=dst[:, :, :planes, :], in_=src[:, :, :planes, :])
+        def weave_x(b, count):
+            dst = x_woven[b][:].rearrange("p (c e t) -> p c t e", e=4, t=PACK)
+            src = x_rows[b][:].rearrange("p t (c e) -> p c t e", e=4)
+            nc.scalar.copy(out=dst[:, :, :count, :], in_=src[:, :, :count, :])
 
-        def x_quant(b):
-            nc.vector.quantize_mx(out=xc[b][:].bitcast(FP8X4), scales=xs[b][:], in_=xil[b][:])
+        def quantise_x(b):
+            nc.vector.quantize_mx(out=x_codes[b][:].bitcast(FP8X4), scales=x_scales[b][:], in_=x_woven[b][:])
 
-        ebank = {}
+        score = {}
 
-        def final_pass(b, c):
+        def score_pass(b, c):
             if b == 0:
-                ebank[c] = psum.tile([P, PJ], F32, name="e%d" % c, tag="bank%d" % c)
+                score[c] = psum.tile([P, PJ], F32, name="e%d" % c, tag="bank%d" % c)
             nc.tensor.matmul_mx(
-                out=ebank[c][:],
-                lhsT=pcodes[b, c].bitcast(FP8X4),
-                lhsT_scale=pscales[b, c],
-                rhs=xc[b][:].bitcast(FP8X4),
-                rhs_scale=xs[b][:],
+                out=score[c][:],
+                lhsT=page_codes[b, c].bitcast(FP8X4),
+                lhsT_scale=page_scales[b, c],
+                rhs=x_codes[b][:].bitcast(FP8X4),
+                rhs_scale=x_scales[b][:],
                 start=(b == 0),
-                stop=(b == 1),
+                stop=(b == PASSES - 1),
             )
 
-        def epilogue(c, j0, j1):
-            mn = ring.tile([P, j1 - j0], F32, name="mn%d_%d" % (c, j0), tag="y", align_bytes=64)
+        def finish(c, j0, j1):
+            bounded = ring.tile([P, j1 - j0], F32, name="mn%d_%d" % (c, j0), tag="y", align_bytes=64)
             nc.vector.tensor_scalar(
-                out=mn[:], in0=ebank[c][:, j0:j1], scalar1=slot_t[:, c : c + 1], scalar2=None, op0=ALU.min
+                out=bounded[:], in0=score[c][:, j0:j1], scalar1=slot_cols[:, c : c + 1], scalar2=None, op0=ALU.min
             )
-            ex = held([P, j1 - j0], F32, "ex%d_%d" % (c, j0), "show%d" % c if j0 == 0 else "gain0")
-            nc.scalar.activation(out=ex[:], in_=mn[:], func=ACT.Exp)
-            nc.sync.dma_start(out=out[c * P : (c + 1) * P, j0:j1], in_=ex[:])
+            result = held([P, j1 - j0], F32, "ex%d_%d" % (c, j0), "show%d" % c if j0 == 0 else "gain0")
+            nc.scalar.activation(out=result[:], in_=bounded[:], func=ACT.Exp)
+            nc.sync.dma_start(out=out[c * P : (c + 1) * P, j0:j1], in_=result[:])
 
         second_product(0)
-        q00a = w1_piece(0, 0, 0, 1, "scalar")
-        q00b = w1_piece(0, 0, 1, 4, "scalar")
-        q00a(0, 1)
-        q10a = w1_piece(1, 0, 0, 1, "vector", "tabs")
-        q10a(0, 1)
-        first_product(0)
-        deal_wd_scales(0, 1, 4, "tabs")
-        q10b = w1_piece(1, 0, 1, 2, "vector")
-        q00b(1, 2, "w1c1000")
-        q10b(1, 2)
+        quantise_w1_a0_t0 = weave_w1(0, 0, 0, 1, nc.scalar.copy)
+        quantise_w1_a0_rest = weave_w1(0, 0, 1, PACK, nc.scalar.copy)
+        quantise_w1_a0_t0(0, 1)
+        weave_w1(1, 0, 0, 1, nc.vector.tensor_copy, "tabs")(0, 1)
+        first_product_squared(0)
+        deal_wd_scales(0, 1, PACK, "tabs")
+        quantise_w1_a1_t1 = weave_w1(1, 0, 1, 2, nc.vector.tensor_copy)
+        last_pass_codes_tag, last_pass_scales_tag = "w1c1000", "w1s1000"
+        quantise_w1_a0_rest(1, 2, last_pass_codes_tag)
+        quantise_w1_a1_t1(1, 2)
         second_product(1)
-        first_product(1)
-        q10c = w1_piece(1, 0, 2, 4, "scalar")
-        sub(0)
-        for n in range(8):
+        first_product_squared(1)
+        quantise_w1_a1_rest = weave_w1(1, 0, 2, PACK, nc.scalar.copy)
+        subtract(0)
+
+        for n in range(ROW_TILES):
             scatter(n)
             if n > 0:
-                floor_scale(n - 1)
+                floor_and_scale(n - 1)
             if n == 0:
-                q00b(2, 4, "w1s1000")
-                q10c(2, 4)
-                for m in (2, 3):
-                    second_product(m)
-                    first_product(m)
+                quantise_w1_a0_rest(2, PACK, last_pass_scales_tag)
+                quantise_w1_a1_rest(2, PACK)
+                for later in range(2, PACK):
+                    second_product(later)
+                    first_product_squared(later)
             if n == 1:
-                for a in range(2):
-                    w1_piece(a, 1, 0, 4, "scalar", "hA" if a == 0 else "hB")(0, 4)
-                for m in range(4, 8):
-                    second_product(m)
-                    first_product(m)
-            if n == 4:
-                x_weave(0, 4)
-                page_quant(0, 0, T2)
-                x_quant(0)
-            if n == 6:
-                x_weave(1, 2)
-            if n + 1 < 8:
-                sub(n + 1)
-            if n < 7:
-                page_round(n, 0, T2)
+                for a, tag in enumerate(("hA", "hB")):
+                    weave_w1(a, 1, 0, PACK, nc.scalar.copy, tag)(0, PACK)
+                for later in range(PACK, ROW_TILES):
+                    second_product(later)
+                    first_product_squared(later)
+            if n == PACK:
+                weave_x(0, PACK)
+                quantise_page(0, 0, T2)
+                quantise_x(0)
+            if n == first_direct:
+                weave_x(1, first_direct - PACK)
+            if n < LAST:
+                subtract(n + 1)
+                weave_page(n, 0, T2)
             else:
-                for c in range(4):
-                    page_round(n, 256 * c, 256 * (c + 1))
+                for m0 in range(0, T2, TAIL_CHUNK):
+                    weave_page(n, m0, m0 + TAIL_CHUNK)
             gather(n)
-        for c in range(8):
-            final_pass(0, c)
-        page_quant(1, 0, 256)
-        floor_scale(7)
-        page_quant(1, 256, 512)
-        x_quant(1)
-        page_quant(1, 512, 768)
-        page_quant(1, 768, 1024)
-        for c in range(8):
-            final_pass(1, c)
-            if c < 7:
-                epilogue(c, 0, PJ)
+
+        for c in range(OUT_TILES):
+            score_pass(0, c)
+        quantise_page(1, 0, TAIL_CHUNK)
+        floor_and_scale(LAST)
+        quantise_page(1, TAIL_CHUNK, 2 * TAIL_CHUNK)
+        quantise_x(1)
+        for m0 in range(2 * TAIL_CHUNK, T2, TAIL_CHUNK):
+            quantise_page(1, m0, m0 + TAIL_CHUNK)
+        for c in range(OUT_TILES):
+            score_pass(1, c)
+            if c < OUT_TILES - 1:
+                finish(c, 0, PJ)
             else:
-                epilogue(c, 0, PJ // 2)
-                epilogue(c, PJ // 2, PJ)
+                finish(c, 0, PJ // 2)
+                finish(c, PJ // 2, PJ)

from contextlib import ExitStack

import concourse.mybir as mybir

H, T, S, T2, PJ = 1024, 2048, 512, 1024, 512
FLOPS = 3221225472

F32 = mybir.dt.float32
BF16 = mybir.dt.bfloat16
I32 = mybir.dt.int32
U32 = mybir.dt.uint32
U16 = mybir.dt.uint16
U8 = mybir.dt.uint8
FP8X4 = mybir.dt.float8_e4m3fn_x4
FP4X4 = mybir.dt.float4_e2m1fn_x4
ALU = mybir.AluOpType
ACT = mybir.ActivationFunctionType

P = 128
PACK = 4
SPAN = P * PACK
PASSES = 2
ROW_TILES = PASSES * PACK
LAST = ROW_TILES - 1
OUT_TILES = T2 // P
QUADRANT = 32
QUADRANT_ORDER = (0, 2, 1, 3)
SQUARES_AHEAD = 4
PAGE_LAG = 3
TAIL_CHUNK = 256


def tile_list_bonsai_vigour_page_kernel(
    tc, tab_words, tab_scales, offs, w1, wd_words, wd_scales, page0, wgs, offs2, offs3, show, low, vec, slot, out
):
    nc = tc.nc
    with ExitStack() as ctx:
        lists = ctx.enter_context(tc.tile_pool(name="lists", bufs=1))
        keep = ctx.enter_context(tc.tile_pool(name="keep", bufs=1))
        ring = ctx.enter_context(tc.tile_pool(name="ring", bufs=3))
        psum = ctx.enter_context(tc.psum_pool(name="psum", bufs=1))

        def held(shape, dtype, name, tag=None):
            return keep.tile(shape, dtype, name=name, tag=tag or name, align_bytes=64)

        scan_list = lists.tile([P, S // 16], U16, name="o1")
        slot_list = lists.tile([P, S // 16], U16, name="o2")
        show_list = lists.tile([P, PJ // 16], U16, name="o3")

        wd_scale_rows = held([P, PASSES * H], U8, "wds_raw")
        tab_scale_rows = held([P, PASSES * T], U8, "tabs")
        nc.vector.memset(tab_scale_rows[:, :T].bitcast(I32), 0)
        nc.gpsimd.memset(tab_scale_rows[:, T:].bitcast(I32), 0)
        nc.vector.memset(wd_scale_rows[:].bitcast(I32), 0)

        tab_word_rows = [held([P, T], U32, "tabw%d" % a) for a in range(PASSES)]
        w1_rows = {
            (a, b): held([P, PACK, SPAN], F32, "w1raw%d%d" % (a, b)) for a in range(PASSES) for b in range(PASSES)
        }
        wd_word_rows = held([P, PASSES * 2 * H], U8, "wdw_raw")
        page = [held([P, T2], F32, "page%d" % n) for n in range(ROW_TILES)]
        show_tile = [held([P, PJ], F32, "show%d" % n) for n in range(ROW_TILES)]
        gain_first = held([P, S], F32, "gain0")
        gain_rest = held([P, PACK - 1, S], F32, "gain123")
        low_cols = held([P, PASSES, PACK], F32, "low_t")
        vec_cols = held([P, PASSES, PACK], F32, "vec_t")
        slot_cols = held([P, OUT_TILES], F32, "slot_t")

        page_rows = page0.rearrange("(b p t) m -> b t p m", b=PASSES, t=PACK)
        show_rows = show.rearrange("(b p t) j -> b t p j", b=PASSES, t=PACK)
        wgs_rows = wgs.rearrange("(p t) j -> p t j", t=PACK)

        def load_tab_words(a):
            nc.sync.dma_start(
                out=tab_word_rows[a][:].bitcast(I32), in_=tab_words[a].rearrange("p n t -> p (n t)").bitcast(I32)
            )

        def load_scale_rows(tile, scales):
            for i in range(PACK):
                nc.sync.dma_start(
                    out=tile[i:P:QUADRANT, :].bitcast(I32).rearrange("q (a c) -> q a c", a=PASSES),
                    in_=scales.bitcast(I32).rearrange("a (q i) c -> i q a c", i=PACK)[i],
                )

        def load_w1(a, b):
            nc.sync.dma_start(
                out=w1_rows[a, b][:],
                in_=w1[SPAN * a : SPAN * (a + 1), SPAN * b : SPAN * (b + 1)].rearrange("(p i) c -> p i c", i=PACK),
            )

        def load_page(n):
            nc.sync.dma_start(out=page[n][:], in_=page_rows[n // PACK, n % PACK])

        def load_show(n):
            nc.sync.dma_start(out=show_tile[n][:], in_=show_rows[n // PACK, n % PACK])

        nc.sync.dma_start(scan_list[:], offs)
        nc.sync.dma_start(
            out=wd_word_rows[:].bitcast(I32).rearrange("p (a c) -> p a c", a=PASSES),
            in_=wd_words.bitcast(I32).rearrange("a p c -> p a c"),
        )
        load_tab_words(0)
        load_scale_rows(tab_scale_rows, tab_scales)
        load_tab_words(1)
        load_w1(0, 0)
        load_scale_rows(wd_scale_rows, wd_scales)
        load_w1(1, 0)
        load_page(0)
        nc.sync.dma_start(slot_list[:], offs2)
        for q in QUADRANT_ORDER:
            nc.sync.dma_start(out=gain_first[QUADRANT * q : QUADRANT * (q + 1), :], in_=wgs_rows[:, 0, :])
        load_show(0)
        nc.sync.dma_start(show_list[:], offs3)
        nc.sync.dma_start(out=low_cols[:], in_=low.rearrange("(b p t) -> p b t", b=PASSES, t=PACK))
        nc.sync.dma_start(out=vec_cols[:], in_=vec.rearrange("(b p t) -> p b t", b=PASSES, t=PACK))
        for q in QUADRANT_ORDER:
            nc.sync.dma_start(out=gain_rest[QUADRANT * q : QUADRANT * (q + 1), :, :], in_=wgs_rows[:, 1:PACK, :])
        load_page(1)
        load_w1(0, 1)
        load_show(1)
        load_page(2)
        load_w1(1, 1)
        load_show(2)
        for n in range(3, ROW_TILES):
            load_page(n)
            load_show(n)
        with nc.allow_non_contiguous_dma(reason="one value a partition"):
            nc.sync.dma_start(out=slot_cols[:], in_=slot.rearrange("(c p) -> p c", p=P))

        v_words = [held([P, S], U32, "vw%d" % a) for a in range(PASSES)]
        v_scales = [held([P, S], U8, "vs%d" % a) for a in range(PASSES)]
        wd_dealt_words = held([P, PASSES * 2 * H], U8, "wdw")
        wd_dealt_scales = {}

        def deal_wd_scales(b, t0, t1, tag):
            dealt = held([P, PASSES, t1 - t0, P], U8, "wds%d%d" % (b, t0), tag)
            src = wd_scale_rows[:].rearrange("p (a b m t) -> p b a t m", a=PASSES, b=PASSES, t=PACK)
            nc.vector.tensor_copy(out=dealt[:], in_=src[:, b, :, t0:t1, :])
            for a in range(PASSES):
                for t in range(t0, t1):
                    wd_dealt_scales[a, b, t] = dealt[:, a, t - t0, :]

        nc.vector.tensor_copy(
            out=wd_dealt_words[:].bitcast(U16).rearrange("p (g t m) -> p g t m", g=PASSES * PASSES, t=PACK),
            in_=wd_word_rows[:].bitcast(U16).rearrange("p (g m t) -> p g t m", g=PASSES * PASSES, t=PACK),
        )
        nc.vector.tensor_copy(v_words[0][:], tab_word_rows[0][:].indirect(scan_list[:]))
        nc.vector.tensor_copy(v_scales[0][:], tab_scale_rows[:, :T].indirect(scan_list[:]))
        nc.vector.tensor_copy(v_scales[1][:], tab_scale_rows[:, T:].indirect(scan_list[:]))
        nc.vector.tensor_copy(v_words[1][:], tab_word_rows[1][:].indirect(scan_list[:]))
        deal_wd_scales(0, 0, 1, "tabw1")
        deal_wd_scales(1, 0, PACK, "tabw0")

        w1_codes = {}
        w1_scales = {}

        def weave_w1(a, b, t0, t1, copy, tag=None):
            count = t1 - t0
            name = "%d%d%d" % (a, b, t0)
            woven = held([P, count * SPAN], BF16, "w1bf" + name, tag)
            if count == 1:
                src = w1_rows[a, b][:].rearrange("p i (m t) -> p t m i", t=PACK)[:, t0, :, :]
                dst = woven[:].rearrange("p (m i) -> p m i", i=PACK)
            else:
                src = w1_rows[a, b][:].rearrange("p i (m e t) -> p m i e t", e=2, t=PACK)[:, :, :, :, t0:t1]
                dst = woven[:].rearrange("p (t m e i) -> p m i e t", t=count, e=2, i=PACK)
            copy(out=dst, in_=src)

            def quantise(u0, u1, codes_tag=None):
                codes = held([P, (u1 - u0) * P], U32, "w1c%s%d" % (name, u0), codes_tag)
                scales = held([P, (u1 - u0) * P], U8, "w1s%s%d" % (name, u0))
                nc.vector.quantize_mx(
                    out=codes[:].bitcast(FP8X4), scales=scales[:], in_=woven[:, (u0 - t0) * SPAN : (u1 - t0) * SPAN]
                )
                for t in range(u0, u1):
                    w1_codes[a, b, t] = codes[:, (t - u0) * P : (t - u0 + 1) * P]
                    w1_scales[a, b, t] = scales[:, (t - u0) * P : (t - u0 + 1) * P]

            return quantise

        second = {}
        squared = {}
        h = {}
        picked = {}

        def second_product(n):
            b, t = divmod(n, PACK)
            second[n] = psum.tile([P, S], F32, name="second%d" % n, tag="bank%d" % (2 * (n % SQUARES_AHEAD) + 1))
            for a in range(PASSES):
                byte0 = 2 * P * ((PASSES * a + b) * PACK + t)
                nc.tensor.matmul_mx(
                    out=second[n][:],
                    lhsT=wd_dealt_words[:, byte0 : byte0 + 2 * P].bitcast(FP4X4),
                    lhsT_scale=wd_dealt_scales[a, b, t],
                    rhs=v_words[a][:].bitcast(FP8X4),
                    rhs_scale=v_scales[a][:],
                    start=(a == 0),
                    stop=(a == PASSES - 1),
                )

        def first_product_squared(n):
            b, t = divmod(n, PACK)
            first = psum.tile([P, S], F32, name="first%d" % n, tag="bank%d" % (2 * (n % SQUARES_AHEAD)))
            for a in range(PASSES):
                nc.tensor.matmul_mx(
                    out=first[:],
                    lhsT=w1_codes[a, b, t].bitcast(FP8X4),
                    lhsT_scale=w1_scales[a, b, t],
                    rhs=v_words[a][:].bitcast(FP8X4),
                    rhs_scale=v_scales[a][:],
                    start=(a == 0),
                    stop=(a == PASSES - 1),
                )
            squared[n] = ring.tile([P, S], F32, name="sq%d" % n, tag="sq", bufs=SQUARES_AHEAD, align_bytes=64)
            nc.scalar.activation(out=squared[n][:], in_=first[:], func=ACT.Square)

        early_h_tags = ("hB", "hB", "show0")

        def subtract(n):
            if n < PAGE_LAG:
                h[n] = held([P, S], F32, "h%d" % n, early_h_tags[n])[:]
            else:
                pair = held([P, 2, S], F32, "hy%d" % n, "page%d" % (n - PAGE_LAG))
                h[n] = pair[:, 0, :]
                picked[n - 1] = pair[:, 1, :]
            nc.vector.tensor_tensor(out=h[n], in0=squared[n][:], in1=second[n][:], op=ALU.subtract)

        def scatter(n):
            t = n % PACK
            gain = gain_first[:] if t == 0 else gain_rest[:, t - 1, :]
            nc.vector.tensor_tensor(page[n][:].indirect(slot_list[:]), h[n], gain, ALU.mult)

        page_woven = [held([P, PACK * T2], BF16, "pgbf%d" % b) for b in range(PASSES)]

        def weave_page(n, m0, m1):
            b, t = divmod(n, PACK)
            dst = page_woven[b][:].rearrange("p (m t) -> p t m", t=PACK)
            nc.scalar.copy(out=dst[:, t, m0:m1], in_=page[n][:, m0:m1])

        page_codes = {}
        page_scales = {}

        def quantise_page(b, m0, m1):
            codes = held([P, m1 - m0], U32, "pc%d_%d" % (b, m0))
            scales = held([P, m1 - m0], U8, "ps%d_%d" % (b, m0))
            nc.vector.quantize_mx(
                out=codes[:].bitcast(FP8X4), scales=scales[:], in_=page_woven[b][:, PACK * m0 : PACK * m1]
            )
            for c in range(m0 // P, m1 // P):
                page_codes[b, c] = codes[:, c * P - m0 : (c + 1) * P - m0]
                page_scales[b, c] = scales[:, c * P - m0 : (c + 1) * P - m0]

        def gather(n):
            if n not in picked:
                picked[n] = held([P, PJ], F32, "y%d" % n, "hA" if n == 0 else None)[:]
            nc.vector.tensor_tensor(picked[n], page[n][:].indirect(show_list[:]), show_tile[n][:], ALU.mult)

        x_rows = [held([P, PACK, PJ], BF16, "xst%d" % b) for b in range(PASSES)]
        x_woven = [held([P, PACK * PJ], BF16, "xil%d" % b) for b in range(PASSES)]
        x_codes = [held([P, PJ], U32, "xc%d" % b) for b in range(PASSES)]
        x_scales = [held([P, PJ], U8, "xs%d" % b) for b in range(PASSES)]
        first_direct = ROW_TILES - 2

        def floor_and_scale(n):
            b, t = divmod(n, PACK)
            places = x_woven[b][:].rearrange("p (j t) -> p t j", t=PACK)
            nc.vector.tensor_scalar(
                out=x_rows[b][:, t, :] if n < first_direct else places[:, t, :],
                in0=picked[n],
                scalar1=low_cols[:, b, t : t + 1],
                scalar2=vec_cols[:, b, t : t + 1],
                op0=ALU.max,
                op1=ALU.mult,
            )

        def weave_x(b, count):
            dst = x_woven[b][:].rearrange("p (c e t) -> p c t e", e=4, t=PACK)
            src = x_rows[b][:].rearrange("p t (c e) -> p c t e", e=4)
            nc.scalar.copy(out=dst[:, :, :count, :], in_=src[:, :, :count, :])

        def quantise_x(b):
            nc.vector.quantize_mx(out=x_codes[b][:].bitcast(FP8X4), scales=x_scales[b][:], in_=x_woven[b][:])

        score = {}

        def score_pass(b, c):
            if b == 0:
                score[c] = psum.tile([P, PJ], F32, name="e%d" % c, tag="bank%d" % c)
            nc.tensor.matmul_mx(
                out=score[c][:],
                lhsT=page_codes[b, c].bitcast(FP8X4),
                lhsT_scale=page_scales[b, c],
                rhs=x_codes[b][:].bitcast(FP8X4),
                rhs_scale=x_scales[b][:],
                start=(b == 0),
                stop=(b == PASSES - 1),
            )

        def finish(c, j0, j1):
            bounded = ring.tile([P, j1 - j0], F32, name="mn%d_%d" % (c, j0), tag="y", align_bytes=64)
            nc.vector.tensor_scalar(
                out=bounded[:], in0=score[c][:, j0:j1], scalar1=slot_cols[:, c : c + 1], scalar2=None, op0=ALU.min
            )
            result = held([P, j1 - j0], F32, "ex%d_%d" % (c, j0), "show%d" % c if j0 == 0 else "gain0")
            nc.scalar.activation(out=result[:], in_=bounded[:], func=ACT.Exp)
            nc.sync.dma_start(out=out[c * P : (c + 1) * P, j0:j1], in_=result[:])

        second_product(0)
        quantise_w1_a0_t0 = weave_w1(0, 0, 0, 1, nc.scalar.copy)
        quantise_w1_a0_rest = weave_w1(0, 0, 1, PACK, nc.scalar.copy)
        quantise_w1_a0_t0(0, 1)
        weave_w1(1, 0, 0, 1, nc.vector.tensor_copy, "tabs")(0, 1)
        first_product_squared(0)
        deal_wd_scales(0, 1, PACK, "tabs")
        quantise_w1_a1_t1 = weave_w1(1, 0, 1, 2, nc.vector.tensor_copy)
        last_pass_codes_tag, last_pass_scales_tag = "w1c1000", "w1s1000"
        quantise_w1_a0_rest(1, 2, last_pass_codes_tag)
        quantise_w1_a1_t1(1, 2)
        second_product(1)
        first_product_squared(1)
        quantise_w1_a1_rest = weave_w1(1, 0, 2, PACK, nc.scalar.copy)
        subtract(0)

        for n in range(ROW_TILES):
            scatter(n)
            if n > 0:
                floor_and_scale(n - 1)
            if n == 0:
                quantise_w1_a0_rest(2, PACK, last_pass_scales_tag)
                quantise_w1_a1_rest(2, PACK)
                for later in range(2, PACK):
                    second_product(later)
                    first_product_squared(later)
            if n == 1:
                for a, tag in enumerate(("hA", "hB")):
                    weave_w1(a, 1, 0, PACK, nc.scalar.copy, tag)(0, PACK)
                for later in range(PACK, ROW_TILES):
                    second_product(later)
                    first_product_squared(later)
            if n == PACK:
                weave_x(0, PACK)
                quantise_page(0, 0, T2)
                quantise_x(0)
            if n == first_direct:
                weave_x(1, first_direct - PACK)
            if n < LAST:
                subtract(n + 1)
                weave_page(n, 0, T2)
            else:
                for m0 in range(0, T2, TAIL_CHUNK):
                    weave_page(n, m0, m0 + TAIL_CHUNK)
            gather(n)

        for c in range(OUT_TILES):
            score_pass(0, c)
        quantise_page(1, 0, TAIL_CHUNK)
        floor_and_scale(LAST)
        quantise_page(1, TAIL_CHUNK, 2 * TAIL_CHUNK)
        quantise_x(1)
        for m0 in range(2 * TAIL_CHUNK, T2, TAIL_CHUNK):
            quantise_page(1, m0, m0 + TAIL_CHUNK)
        for c in range(OUT_TILES):
            score_pass(1, c)
            if c < OUT_TILES - 1:
                finish(c, 0, PJ)
            else:
                finish(c, 0, PJ // 2)
                finish(c, PJ // 2, PJ)
